import numpy as np
import ml_dtypes


def mxq(x, axis, fmt="e4m3"):
    dtype, down = {"e4m3": (ml_dtypes.float8_e4m3fn, 7), "e5m2": (ml_dtypes.float8_e5m2, 14)}[fmt]
    v = np.moveaxis(np.asarray(x, np.float32).astype(ml_dtypes.bfloat16).astype(np.float64), axis, -1)
    blocks = v.reshape(v.shape[:-1] + (-1, 32))
    amax = np.abs(blocks).max(-1, keepdims=True)
    byte = np.maximum(np.where(amax > 0, np.frexp(amax)[1] - 1 + 127, 0) - down, 1)
    scale = np.exp2(byte - 127.0)
    codes = (blocks / scale).astype(np.float32).astype(dtype).astype(np.float64)
    return np.moveaxis((codes * scale).reshape(v.shape), -1, axis)


WIDE = False


def mx_kscale(k):
    if not WIDE:
        return np.ones(k)
    levels = np.array([10, -10, 5, -5, 0])
    if k % 512:
        return np.exp2(np.random.permutation(np.resize(levels, k // 32))).repeat(32)
    a = np.empty((k // 512, 16))
    for p in range(k // 512):
        a[p, :8] = np.random.permutation(np.resize(levels, 8))
        for g in range(8):
            far = levels[np.abs(levels - a[p, g]) >= 10]
            a[p, g + 8] = far[np.random.randint(len(far))]
    return np.exp2(a.ravel()).repeat(32)


BF16 = ml_dtypes.bfloat16


def bf(x):
    return np.asarray(x, np.float32).astype(BF16)


def f64(x):
    return np.asarray(x).astype(np.float64)


E2M1 = np.array([0.0, 0.5, 1.0, 1.5, 2.0, 3.0, 4.0, 6.0, -0.0, -0.5, -1.0, -1.5, -2.0, -3.0, -4.0, -6.0])


def pack_weight(w, fmt):
    k, n = w.shape
    w = f64(bf(w)).reshape(k // 32, 32, n)
    amax = np.abs(w).max(1)
    if fmt == "e4m3":
        byte = np.frexp(amax)[1] - 1 + 127 - 7
    else:
        mant, ex = np.frexp(amax / 6.0)
        byte = np.where(mant > 0.5, ex, ex - 1) + 127
    byte = np.clip(np.where(amax > 0, byte, 1), 1, 254)
    scaled = (w * np.exp2(127.0 - byte)[:, None, :]).reshape(k, n).astype(np.float32)
    by_word = np.ascontiguousarray(scaled.reshape(k // 512, 128, 4, n).transpose(0, 1, 3, 2))
    if fmt == "e4m3":
        words = by_word.astype(ml_dtypes.float8_e4m3fn).view(np.uint8)
    else:
        c = by_word.astype(ml_dtypes.float4_e2m1fn).view(np.uint8) & 0xF
        words = c[..., 0::2] | (c[..., 1::2] << 4)
    return np.ascontiguousarray(words), np.ascontiguousarray(byte.astype(np.uint8).reshape(k // 512, 16, n))


def unpack_weight(words, scales, fmt):
    g, p, n, _ = words.shape
    if fmt == "e4m3":
        vals = np.ascontiguousarray(words).view(ml_dtypes.float8_e4m3fn).astype(np.float64)
    else:
        nib = np.empty((g, p, n, 4), np.uint8)
        nib[..., 0::2] = words & 0xF
        nib[..., 1::2] = words >> 4
        vals = E2M1[nib]
    vals = vals * np.repeat(np.exp2(scales.astype(np.float64) - 127.0), 8, axis=1)[..., None]
    return vals.transpose(0, 1, 3, 2).reshape(g * 512, n)
def pack4(w):
    words, scales = pack_weight(w, "e2m1")
    return words.reshape(words.shape[0], 128, -1), scales


def unpack4(words, scales):
    return unpack_weight(words.reshape(words.shape[0], 128, -1, 2), scales, "e2m1")


G, R, K = 8, 1024, 512

B, C = -4.7750, 2.0315
D = 0.35


def setup_inputs():
    s = mx_kscale(K)
    x = np.random.standard_normal((G, R, K))
    a = np.swapaxes(x, 1, 2) @ x * (D / R)
    a = a / s[:, None] * s
    a_words, a_scales = pack4(a.reshape(G * K, K))
    return {"x": bf(x * s),
            "a_words": a_words,
            "a_scales": a_scales,
            "step": bf(C * (1 + 0.1 * np.random.standard_normal((G, K))) / s)}


def reference(x, a_words, a_scales, step):
    x = f64(x)
    a = unpack4(a_words, a_scales).reshape(G, K, K)
    y = mxq(x, 2, "e4m3") @ a
    h = (B / C) * x + y
    z = mxq(h, 2, "e4m3") @ a
    return z * f64(step)[:, None, :]

@@ -1,0 +1,269 @@
+from contextlib import ExitStack
+
+import concourse.mybir as mybir
+from concourse.masks import make_identity
+
+G, R, K = 8, 1024, 512
+B_COEF, C_COEF = -4.7750, 2.0315
+FLOPS = 2 * 2 * G * R * K * K
+
+F32 = mybir.dt.float32
+BF16 = mybir.dt.bfloat16
+I32 = mybir.dt.int32
+U32 = mybir.dt.uint32
+U8 = mybir.dt.uint8
+FP8X4 = mybir.dt.float8_e4m3fn_x4
+FP4X4 = mybir.dt.float4_e2m1fn_x4
+MULT = mybir.AluOpType.mult
+ADD = mybir.AluOpType.add
+
+P = 128
+PACK = 4
+TILES = 4
+STEPS_PER_LAYER = R // (P * TILES)
+STEPS = G * STEPS_PER_LAYER
+WIDTH = TILES * K
+GP_COLS = 1216
+LOAD_AHEAD = 5
+
+
+def tile_muon_quintic_tail_s14_kernel(tc, x, a_words, a_scales, step, out):
+    nc = tc.nc
+    with ExitStack() as ctx:
+        keep = ctx.enter_context(tc.tile_pool(name="keep", bufs=1))
+        flow = ctx.enter_context(tc.tile_pool(name="flow", bufs=3))
+        psum = ctx.enter_context(tc.psum_pool(name="psum", bufs=3))
+        ctx.enter_context(tc.manual_schedule())
+
+        def step_rows(t, s):
+            l, h = divmod(s, STEPS_PER_LAYER)
+            return t[l, h * P * TILES : (h + 1) * P * TILES, :].rearrange("(p j) k -> p (j k)", j=TILES)
+
+        plane = keep.tile([P, G * K], U8, align_bytes=64)
+        plane_perm = keep.tile([P, G * K], U8, align_bytes=64)
+        step_rows_sb = keep.tile([P, K], BF16, align_bytes=64)
+        ident = keep.tile([P, P], F32, align_bytes=64)
+        ident_bf = keep.tile([P, P], BF16, align_bytes=64)
+
+        x_halves, words, words_perm, step_bc = {}, {}, {}, {}
+        xt, x_codes, x_scales, hz, h_codes, h_scales, y_banks, z_sb = {}, {}, {}, {}, {}, {}, {}, {}
+
+        def load_x_half(s, half):
+            t = keep.tile([P, 2 * K], BF16, name="x_first%d" % half)
+            nc.sync.dma_start(out=t[:], in_=step_rows(x, s)[:, half * 2 * K : (half + 1) * 2 * K])
+            x_halves[s, half] = t[:]
+
+        def load_x(s):
+            t = flow.tile([P, WIDTH], BF16, name="x_sb", bufs=LOAD_AHEAD + 1)
+            nc.sync.dma_start(out=t[:], in_=step_rows(x, s))
+            x_halves[s, 0] = t[:, 0 : 2 * K]
+            x_halves[s, 1] = t[:, 2 * K : 4 * K]
+
+        def load_words(l):
+            t = keep.tile([P, 2 * K], U8, name="a_nat%d" % l, align_bytes=64)
+            nc.sync.dma_start(out=t[:].bitcast(I32), in_=a_words[l].bitcast(I32))
+            words[l] = t
+
+        def permute_words(l):
+            t = keep.tile([P, 2 * K], U8, name="a_perm%d" % l, align_bytes=64)
+            nc.vector.tensor_copy(
+                out=t[:].rearrange("p (t c i b) -> p c t i b", t=PACK, i=8, b=2),
+                in_=words[l][:].rearrange("p (c i t b) -> p c t i b", t=PACK, i=8, b=2),
+            )
+            words_perm[l] = t
+
+        def permute_scales(l0, l1):
+            cols = slice(l0 * K, l1 * K)
+            nc.vector.tensor_copy(
+                out=plane_perm[:, cols].rearrange("p (l t c i) -> p l c t i", l=l1 - l0, t=PACK, i=16),
+                in_=plane[:, cols].rearrange("p (l c i t) -> p l c t i", l=l1 - l0, t=PACK, i=16),
+            )
+
+        def spread_step(pair):
+            bank = psum.tile([P, 2 * K], BF16, name="z_bank")
+            for e in range(2):
+                l = 2 * pair + e
+                nc.tensor.matmul(
+                    out=bank[:, e * K : (e + 1) * K],
+                    lhsT=ident_bf[:, l : l + 1].to_broadcast([P, P]),
+                    rhs=step_rows_sb[:],
+                    start=True,
+                    stop=True,
+                )
+            t = keep.tile([P, 2 * K], BF16, name="step_bc%d" % pair)
+            nc.scalar.copy(out=t[:], in_=bank[:])
+            step_bc[2 * pair] = t[:, 0:K]
+            step_bc[2 * pair + 1] = t[:, K : 2 * K]
+
+        def turn_x(s):
+            t = flow.tile([P, WIDTH], BF16, name="x_t", bufs=4, align_bytes=64)
+            xt[s] = t
+            for half in range(2):
+                src = x_halves[s, half].bitcast(F32)
+                bank = psum.tile([P, 2, 2, P], F32, name="t_bank", bufs=2)
+                for j in range(2):
+                    for u in range(2):
+                        nc.tensor.transpose(bank[:, j, u, :], src[:, 256 * j + u : 256 * (j + 1) : 2], ident[:])
+                dst = t[:, half * 2 * K : (half + 1) * 2 * K].bitcast(F32)
+                nc.scalar.copy(
+                    out=dst.rearrange("p (j r u) -> p j r u", j=2, u=2),
+                    in_=bank[:].rearrange("p j u r -> p j r u"),
+                )
+
+        def quantize_x(s):
+            codes = flow.tile([P, K], U32, name="x_codes", align_bytes=64)
+            scales = flow.tile([P, K], U8, name="x_scales", align_bytes=64)
+            nc.vector.quantize_mx(out=codes[:].bitcast(FP8X4), scales=scales[:], in_=xt[s][:])
+            x_codes[s], x_scales[s] = codes, scales
+
+        def quantize_h(s):
+            codes = flow.tile([P, K], U32, name="h_codes", align_bytes=64)
+            scales = flow.tile([P, K], U8, name="h_scales", align_bytes=64)
+            nc.vector.quantize_mx(out=codes[:].bitcast(FP8X4), scales=scales[:], in_=hz[s][:, 0 : WIDTH // 2].bitcast(BF16))
+            h_codes[s], h_scales[s] = codes, scales
+
+        def first_product(s, j):
+            l = s // STEPS_PER_LAYER
+            bank = psum.tile([P, K], F32, name="y_bank")
+            rows = slice(j * P, (j + 1) * P)
+            for t in range(PACK):
+                nc.tensor.matmul_mx(
+                    out=bank[:, t * P : (t + 1) * P],
+                    lhsT=words_perm[l][:, 2 * t * P : 2 * (t + 1) * P].bitcast(FP4X4),
+                    lhsT_scale=plane_perm[:, l * K + t * P : l * K + (t + 1) * P],
+                    rhs=x_codes[s][:, rows].bitcast(FP8X4),
+                    rhs_scale=x_scales[s][:, rows],
+                    start=True,
+                    stop=True,
+                )
+            y_banks[s, j] = bank
+
+        def combine(s, j):
+            if j == 0:
+                hz[s] = flow.tile([P, max(GP_COLS, WIDTH // 2)], F32, name="h_then_out", bufs=4, align_bytes=64)
+            h = hz[s][:, 0 : WIDTH // 2].bitcast(BF16)
+            cols = slice(j * K, (j + 1) * K)
+            nc.vector.scalar_tensor_tensor(
+                out=h[:, cols].rearrange("p (r t) -> p r t", t=PACK),
+                in0=xt[s][:, cols].rearrange("p (r t) -> p r t", t=PACK),
+                scalar=B_COEF / C_COEF,
+                in1=y_banks[s, j][:].rearrange("p (t r) -> p r t", t=PACK),
+                op0=MULT,
+                op1=ADD,
+            )
+
+        def second_product(s, j):
+            l = s // STEPS_PER_LAYER
+            bank = psum.tile([P, K], F32, name="z_bank")
+            rows = slice(j * P, (j + 1) * P)
+            nc.tensor.matmul_mx(
+                out=bank[:],
+                lhsT=h_codes[s][:, rows].bitcast(FP8X4),
+                lhsT_scale=h_scales[s][:, rows],
+                rhs=words[l][:].bitcast(FP4X4),
+                rhs_scale=plane[:, l * K : (l + 1) * K],
+                start=True,
+                stop=True,
+            )
+            return bank
+
+        def gpsimd_scale(s, dst):
+            l = s // STEPS_PER_LAYER
+            whole = GP_COLS // K
+            nc.gpsimd.tensor_tensor(
+                out=dst[:, 0 : whole * K].rearrange("p (j n) -> p j n", j=whole),
+                in0=z_sb[s][:, 0 : whole * K].rearrange("p (j n) -> p j n", j=whole),
+                in1=step_bc[l].unsqueeze(1).to_broadcast([P, whole, K]),
+                op=MULT,
+            )
+            if GP_COLS > whole * K:
+                nc.gpsimd.tensor_tensor(
+                    out=dst[:, whole * K : GP_COLS],
+                    in0=z_sb[s][:, whole * K : GP_COLS],
+                    in1=step_bc[l][:, 0 : GP_COLS - whole * K],
+                    op=MULT,
+                )
+
+        nc.vector.memset(plane[:].bitcast(I32), 0)
+        make_identity(nc, ident[:])
+        nc.gpsimd.memset(step_rows_sb[:].bitcast(I32), 0)
+        nc.scalar.copy(out=ident_bf[:], in_=ident[:])
+        load_x_half(0, 0)
+        plane_rows = plane[:].bitcast(I32).rearrange("p (l n) -> p l n", l=G)
+        for r in range(4):
+            nc.sync.dma_start(out=plane_rows[r:P:32], in_=a_scales.bitcast(I32)[:, r:16:4, :].rearrange("l q n -> q l n"))
+        load_words(0)
+        load_x_half(0, 1)
+        load_words(1)
+        load_x(1)
+        nc.sync.dma_start(out=step_rows_sb[0:G, :], in_=step)
+        load_words(2)
+        turn_x(0)
+        permute_words(0)
+        permute_words(1)
+        permute_scales(0, G // 2)
+
+        for i in range(-2, STEPS + 1):
+            if i + 4 < STEPS:
+                load_x(i + 4)
+            if i % 2 == 0 and 3 <= i // 2 + 3 < G:
+                load_words(i // 2 + 3)
+            if i % 2 == 1 and 3 <= (i + 3) // 2 < G:
+                permute_words((i + 3) // 2)
+            if i + 2 < STEPS:
+                quantize_x(i + 2)
+            if i == -2:
+                permute_scales(G // 2, G)
+                permute_words(2)
+            if 0 <= i < STEPS:
+                quantize_h(i)
+            if i + 3 < STEPS:
+                turn_x(i + 3)
+            if 1 <= i < STEPS:
+                gpsimd_scale(i - 1, hz[i])
+            nxt = i + 1
+            has_h = 0 <= nxt < STEPS
+            has_z = 0 <= i < STEPS
+            last = i == STEPS - 1
+            if has_h:
+                combine(nxt, 0)
+            if has_z and not last:
+                z_sb[i] = flow.tile([P, GP_COLS], F32, name="z_sb")
+                for j in range(2):
+                    bank = second_product(i, j)
+                    nc.scalar.copy(out=z_sb[i][:, j * K : (j + 1) * K], in_=bank[:])
+            if i == -1:
+                spread_step(2)
+                spread_step(3)
+            if has_h:
+                first_product(nxt, 3)
+                for j in range(1, TILES):
+                    combine(nxt, j)
+            if has_z and not last:
+                l = i // STEPS_PER_LAYER
+                part = GP_COLS - 2 * K
+                bank2 = second_product(i, 2)
+                if part:
+                    nc.scalar.copy(out=z_sb[i][:, 2 * K : GP_COLS], in_=bank2[:, 0:part])
+                bank3 = second_product(i, 3)
+                res = flow.tile([P, WIDTH - GP_COLS], F32, name="res")
+                nc.vector.tensor_tensor(out=res[:, 0 : K - part], in0=bank2[:, part:K], in1=step_bc[l][:, part:K], op=MULT)
+                nc.vector.tensor_tensor(out=res[:, K - part : 2 * K - part], in0=bank3[:], in1=step_bc[l], op=MULT)
+            if 0 <= i + 2 < STEPS:
+                for j in range(3):
+                    first_product(i + 2, j)
+            if i == -2:
+                spread_step(0)
+                spread_step(1)
+            if last:
+                for j in range(TILES):
+                    bank = second_product(i, j)
+                    res_j = flow.tile([P, K], F32, name="res_last", bufs=TILES)
+                    nc.vector.tensor_tensor(out=res_j[:], in0=bank[:], in1=step_bc[G - 1], op=MULT)
+                    if j == 2:
+                        nc.sync.dma_start(out=step_rows(out, i - 1)[:, 0:GP_COLS], in_=hz[i][:, 0:GP_COLS])
+                    nc.sync.dma_start(out=step_rows(out, i)[:, j * K : (j + 1) * K], in_=res_j[:])
+            elif has_z:
+                if i >= 1:
+                    nc.sync.dma_start(out=step_rows(out, i - 1)[:, 0:GP_COLS], in_=hz[i][:, 0:GP_COLS])
+                nc.sync.dma_start(out=step_rows(out, i)[:, GP_COLS:WIDTH], in_=res[:])

@@ -23,8 +23,8 @@ TILES = 4
 STEPS_PER_LAYER = R // (P * TILES)
 STEPS = G * STEPS_PER_LAYER
 WIDTH = TILES * K
-GP_COLS = 1216
-LOAD_AHEAD = 5
+GP_COLS = 1152
+LOAD_AHEAD = 7
 
 
 def tile_muon_quintic_tail_s14_kernel(tc, x, a_words, a_scales, step, out):
@@ -90,13 +90,13 @@ def tile_muon_quintic_tail_s14_kernel(tc, x, a_words, a_scales, step, out):
                     start=True,
                     stop=True,
                 )
-            t = keep.tile([P, 2 * K], BF16, name="step_bc%d" % pair)
+            t = keep.tile([P, 2 * K], F32, name="step_bc%d" % pair)
             nc.scalar.copy(out=t[:], in_=bank[:])
             step_bc[2 * pair] = t[:, 0:K]
             step_bc[2 * pair + 1] = t[:, K : 2 * K]
 
         def turn_x(s):
-            t = flow.tile([P, WIDTH], BF16, name="x_t", bufs=4, align_bytes=64)
+            t = flow.tile([P, WIDTH], BF16, name="x_t", bufs=5, align_bytes=64)
             xt[s] = t
             for half in range(2):
                 src = x_halves[s, half].bitcast(F32)
@@ -198,14 +198,17 @@ def tile_muon_quintic_tail_s14_kernel(tc, x, a_words, a_scales, step, out):
         load_x(1)
         nc.sync.dma_start(out=step_rows_sb[0:G, :], in_=step)
         load_words(2)
+        for s in range(2, LOAD_AHEAD - 2):
+            load_x(s)
         turn_x(0)
+        turn_x(1)
         permute_words(0)
         permute_words(1)
         permute_scales(0, G // 2)
 
         for i in range(-2, STEPS + 1):
-            if i + 4 < STEPS:
-                load_x(i + 4)
+            if i + LOAD_AHEAD < STEPS:
+                load_x(i + LOAD_AHEAD)
             if i % 2 == 0 and 3 <= i // 2 + 3 < G:
                 load_words(i // 2 + 3)
             if i % 2 == 1 and 3 <= (i + 3) // 2 < G:
@@ -217,8 +220,8 @@ def tile_muon_quintic_tail_s14_kernel(tc, x, a_words, a_scales, step, out):
                 permute_words(2)
             if 0 <= i < STEPS:
                 quantize_h(i)
-            if i + 3 < STEPS:
-                turn_x(i + 3)
+            if 0 <= i < G // 2 - 1:
+                spread_step(i + 1)
             if 1 <= i < STEPS:
                 gpsimd_scale(i - 1, hz[i])
             nxt = i + 1
@@ -232,9 +235,6 @@ def tile_muon_quintic_tail_s14_kernel(tc, x, a_words, a_scales, step, out):
                 for j in range(2):
                     bank = second_product(i, j)
                     nc.scalar.copy(out=z_sb[i][:, j * K : (j + 1) * K], in_=bank[:])
-            if i == -1:
-                spread_step(2)
-                spread_step(3)
             if has_h:
                 first_product(nxt, 3)
                 for j in range(1, TILES):
@@ -249,12 +249,14 @@ def tile_muon_quintic_tail_s14_kernel(tc, x, a_words, a_scales, step, out):
                 res = flow.tile([P, WIDTH - GP_COLS], F32, name="res")
                 nc.vector.tensor_tensor(out=res[:, 0 : K - part], in0=bank2[:, part:K], in1=step_bc[l][:, part:K], op=MULT)
                 nc.vector.tensor_tensor(out=res[:, K - part : 2 * K - part], in0=bank3[:], in1=step_bc[l], op=MULT)
+            if i >= -1 and i + 4 < STEPS:
+                turn_x(i + 4)
             if 0 <= i + 2 < STEPS:
                 for j in range(3):
                     first_product(i + 2, j)
             if i == -2:
                 spread_step(0)
-                spread_step(1)
+                turn_x(2)
             if last:
                 for j in range(TILES):
                     bank = second_product(i, j)

from contextlib import ExitStack

import concourse.mybir as mybir
from concourse.masks import make_identity

G, R, K = 8, 1024, 512
B_COEF, C_COEF = -4.7750, 2.0315
FLOPS = 2 * 2 * G * R * K * K

F32 = mybir.dt.float32
BF16 = mybir.dt.bfloat16
I32 = mybir.dt.int32
U32 = mybir.dt.uint32
U8 = mybir.dt.uint8
FP8X4 = mybir.dt.float8_e4m3fn_x4
FP4X4 = mybir.dt.float4_e2m1fn_x4
MULT = mybir.AluOpType.mult
ADD = mybir.AluOpType.add

P = 128
PACK = 4
TILES = 4
STEPS_PER_LAYER = R // (P * TILES)
STEPS = G * STEPS_PER_LAYER
WIDTH = TILES * K
GP_COLS = 1152
LOAD_AHEAD = 7


def tile_muon_quintic_tail_s14_kernel(tc, x, a_words, a_scales, step, out):
    nc = tc.nc
    with ExitStack() as ctx:
        keep = ctx.enter_context(tc.tile_pool(name="keep", bufs=1))
        flow = ctx.enter_context(tc.tile_pool(name="flow", bufs=3))
        psum = ctx.enter_context(tc.psum_pool(name="psum", bufs=3))
        ctx.enter_context(tc.manual_schedule())

        def step_rows(t, s):
            l, h = divmod(s, STEPS_PER_LAYER)
            return t[l, h * P * TILES : (h + 1) * P * TILES, :].rearrange("(p j) k -> p (j k)", j=TILES)

        plane = keep.tile([P, G * K], U8, align_bytes=64)
        plane_perm = keep.tile([P, G * K], U8, align_bytes=64)
        step_rows_sb = keep.tile([P, K], BF16, align_bytes=64)
        ident = keep.tile([P, P], F32, align_bytes=64)
        ident_bf = keep.tile([P, P], BF16, align_bytes=64)

        x_halves, words, words_perm, step_bc = {}, {}, {}, {}
        xt, x_codes, x_scales, hz, h_codes, h_scales, y_banks, z_sb = {}, {}, {}, {}, {}, {}, {}, {}

        def load_x_half(s, half):
            t = keep.tile([P, 2 * K], BF16, name="x_first%d" % half)
            nc.sync.dma_start(out=t[:], in_=step_rows(x, s)[:, half * 2 * K : (half + 1) * 2 * K])
            x_halves[s, half] = t[:]

        def load_x(s):
            t = flow.tile([P, WIDTH], BF16, name="x_sb", bufs=LOAD_AHEAD + 1)
            nc.sync.dma_start(out=t[:], in_=step_rows(x, s))
            x_halves[s, 0] = t[:, 0 : 2 * K]
            x_halves[s, 1] = t[:, 2 * K : 4 * K]

        def load_words(l):
            t = keep.tile([P, 2 * K], U8, name="a_nat%d" % l, align_bytes=64)
            nc.sync.dma_start(out=t[:].bitcast(I32), in_=a_words[l].bitcast(I32))
            words[l] = t

        def permute_words(l):
            t = keep.tile([P, 2 * K], U8, name="a_perm%d" % l, align_bytes=64)
            nc.vector.tensor_copy(
                out=t[:].rearrange("p (t c i b) -> p c t i b", t=PACK, i=8, b=2),
                in_=words[l][:].rearrange("p (c i t b) -> p c t i b", t=PACK, i=8, b=2),
            )
            words_perm[l] = t

        def permute_scales(l0, l1):
            cols = slice(l0 * K, l1 * K)
            nc.vector.tensor_copy(
                out=plane_perm[:, cols].rearrange("p (l t c i) -> p l c t i", l=l1 - l0, t=PACK, i=16),
                in_=plane[:, cols].rearrange("p (l c i t) -> p l c t i", l=l1 - l0, t=PACK, i=16),
            )

        def spread_step(pair):
            bank = psum.tile([P, 2 * K], BF16, name="z_bank")
            for e in range(2):
                l = 2 * pair + e
                nc.tensor.matmul(
                    out=bank[:, e * K : (e + 1) * K],
                    lhsT=ident_bf[:, l : l + 1].to_broadcast([P, P]),
                    rhs=step_rows_sb[:],
                    start=True,
                    stop=True,
                )
            t = keep.tile([P, 2 * K], F32, name="step_bc%d" % pair)
            nc.scalar.copy(out=t[:], in_=bank[:])
            step_bc[2 * pair] = t[:, 0:K]
            step_bc[2 * pair + 1] = t[:, K : 2 * K]

        def turn_x(s):
            t = flow.tile([P, WIDTH], BF16, name="x_t", bufs=5, align_bytes=64)
            xt[s] = t
            for half in range(2):
                src = x_halves[s, half].bitcast(F32)
                bank = psum.tile([P, 2, 2, P], F32, name="t_bank", bufs=2)
                for j in range(2):
                    for u in range(2):
                        nc.tensor.transpose(bank[:, j, u, :], src[:, 256 * j + u : 256 * (j + 1) : 2], ident[:])
                dst = t[:, half * 2 * K : (half + 1) * 2 * K].bitcast(F32)
                nc.scalar.copy(
                    out=dst.rearrange("p (j r u) -> p j r u", j=2, u=2),
                    in_=bank[:].rearrange("p j u r -> p j r u"),
                )

        def quantize_x(s):
            codes = flow.tile([P, K], U32, name="x_codes", align_bytes=64)
            scales = flow.tile([P, K], U8, name="x_scales", align_bytes=64)
            nc.vector.quantize_mx(out=codes[:].bitcast(FP8X4), scales=scales[:], in_=xt[s][:])
            x_codes[s], x_scales[s] = codes, scales

        def quantize_h(s):
            codes = flow.tile([P, K], U32, name="h_codes", align_bytes=64)
            scales = flow.tile([P, K], U8, name="h_scales", align_bytes=64)
            nc.vector.quantize_mx(out=codes[:].bitcast(FP8X4), scales=scales[:], in_=hz[s][:, 0 : WIDTH // 2].bitcast(BF16))
            h_codes[s], h_scales[s] = codes, scales

        def first_product(s, j):
            l = s // STEPS_PER_LAYER
            bank = psum.tile([P, K], F32, name="y_bank")
            rows = slice(j * P, (j + 1) * P)
            for t in range(PACK):
                nc.tensor.matmul_mx(
                    out=bank[:, t * P : (t + 1) * P],
                    lhsT=words_perm[l][:, 2 * t * P : 2 * (t + 1) * P].bitcast(FP4X4),
                    lhsT_scale=plane_perm[:, l * K + t * P : l * K + (t + 1) * P],
                    rhs=x_codes[s][:, rows].bitcast(FP8X4),
                    rhs_scale=x_scales[s][:, rows],
                    start=True,
                    stop=True,
                )
            y_banks[s, j] = bank

        def combine(s, j):
            if j == 0:
                hz[s] = flow.tile([P, max(GP_COLS, WIDTH // 2)], F32, name="h_then_out", bufs=4, align_bytes=64)
            h = hz[s][:, 0 : WIDTH // 2].bitcast(BF16)
            cols = slice(j * K, (j + 1) * K)
            nc.vector.scalar_tensor_tensor(
                out=h[:, cols].rearrange("p (r t) -> p r t", t=PACK),
                in0=xt[s][:, cols].rearrange("p (r t) -> p r t", t=PACK),
                scalar=B_COEF / C_COEF,
                in1=y_banks[s, j][:].rearrange("p (t r) -> p r t", t=PACK),
                op0=MULT,
                op1=ADD,
            )

        def second_product(s, j):
            l = s // STEPS_PER_LAYER
            bank = psum.tile([P, K], F32, name="z_bank")
            rows = slice(j * P, (j + 1) * P)
            nc.tensor.matmul_mx(
                out=bank[:],
                lhsT=h_codes[s][:, rows].bitcast(FP8X4),
                lhsT_scale=h_scales[s][:, rows],
                rhs=words[l][:].bitcast(FP4X4),
                rhs_scale=plane[:, l * K : (l + 1) * K],
                start=True,
                stop=True,
            )
            return bank

        def gpsimd_scale(s, dst):
            l = s // STEPS_PER_LAYER
            whole = GP_COLS // K
            nc.gpsimd.tensor_tensor(
                out=dst[:, 0 : whole * K].rearrange("p (j n) -> p j n", j=whole),
                in0=z_sb[s][:, 0 : whole * K].rearrange("p (j n) -> p j n", j=whole),
                in1=step_bc[l].unsqueeze(1).to_broadcast([P, whole, K]),
                op=MULT,
            )
            if GP_COLS > whole * K:
                nc.gpsimd.tensor_tensor(
                    out=dst[:, whole * K : GP_COLS],
                    in0=z_sb[s][:, whole * K : GP_COLS],
                    in1=step_bc[l][:, 0 : GP_COLS - whole * K],
                    op=MULT,
                )

        nc.vector.memset(plane[:].bitcast(I32), 0)
        make_identity(nc, ident[:])
        nc.gpsimd.memset(step_rows_sb[:].bitcast(I32), 0)
        nc.scalar.copy(out=ident_bf[:], in_=ident[:])
        load_x_half(0, 0)
        plane_rows = plane[:].bitcast(I32).rearrange("p (l n) -> p l n", l=G)
        for r in range(4):
            nc.sync.dma_start(out=plane_rows[r:P:32], in_=a_scales.bitcast(I32)[:, r:16:4, :].rearrange("l q n -> q l n"))
        load_words(0)
        load_x_half(0, 1)
        load_words(1)
        load_x(1)
        nc.sync.dma_start(out=step_rows_sb[0:G, :], in_=step)
        load_words(2)
        for s in range(2, LOAD_AHEAD - 2):
            load_x(s)
        turn_x(0)
        turn_x(1)
        permute_words(0)
        permute_words(1)
        permute_scales(0, G // 2)

        for i in range(-2, STEPS + 1):
            if i + LOAD_AHEAD < STEPS:
                load_x(i + LOAD_AHEAD)
            if i % 2 == 0 and 3 <= i // 2 + 3 < G:
                load_words(i // 2 + 3)
            if i % 2 == 1 and 3 <= (i + 3) // 2 < G:
                permute_words((i + 3) // 2)
            if i + 2 < STEPS:
                quantize_x(i + 2)
            if i == -2:
                permute_scales(G // 2, G)
                permute_words(2)
            if 0 <= i < STEPS:
                quantize_h(i)
            if 0 <= i < G // 2 - 1:
                spread_step(i + 1)
            if 1 <= i < STEPS:
                gpsimd_scale(i - 1, hz[i])
            nxt = i + 1
            has_h = 0 <= nxt < STEPS
            has_z = 0 <= i < STEPS
            last = i == STEPS - 1
            if has_h:
                combine(nxt, 0)
            if has_z and not last:
                z_sb[i] = flow.tile([P, GP_COLS], F32, name="z_sb")
                for j in range(2):
                    bank = second_product(i, j)
                    nc.scalar.copy(out=z_sb[i][:, j * K : (j + 1) * K], in_=bank[:])
            if has_h:
                first_product(nxt, 3)
                for j in range(1, TILES):
                    combine(nxt, j)
            if has_z and not last:
                l = i // STEPS_PER_LAYER
                part = GP_COLS - 2 * K
                bank2 = second_product(i, 2)
                if part:
                    nc.scalar.copy(out=z_sb[i][:, 2 * K : GP_COLS], in_=bank2[:, 0:part])
                bank3 = second_product(i, 3)
                res = flow.tile([P, WIDTH - GP_COLS], F32, name="res")
                nc.vector.tensor_tensor(out=res[:, 0 : K - part], in0=bank2[:, part:K], in1=step_bc[l][:, part:K], op=MULT)
                nc.vector.tensor_tensor(out=res[:, K - part : 2 * K - part], in0=bank3[:], in1=step_bc[l], op=MULT)
            if i >= -1 and i + 4 < STEPS:
                turn_x(i + 4)
            if 0 <= i + 2 < STEPS:
                for j in range(3):
                    first_product(i + 2, j)
            if i == -2:
                spread_step(0)
                turn_x(2)
            if last:
                for j in range(TILES):
                    bank = second_product(i, j)
                    res_j = flow.tile([P, K], F32, name="res_last", bufs=TILES)
                    nc.vector.tensor_tensor(out=res_j[:], in0=bank[:], in1=step_bc[G - 1], op=MULT)
                    if j == 2:
                        nc.sync.dma_start(out=step_rows(out, i - 1)[:, 0:GP_COLS], in_=hz[i][:, 0:GP_COLS])
                    nc.sync.dma_start(out=step_rows(out, i)[:, j * K : (j + 1) * K], in_=res_j[:])
            elif has_z:
                if i >= 1:
                    nc.sync.dma_start(out=step_rows(out, i - 1)[:, 0:GP_COLS], in_=hz[i][:, 0:GP_COLS])
                nc.sync.dma_start(out=step_rows(out, i)[:, GP_COLS:WIDTH], in_=res[:])
